import numpy as np
import ml_dtypes


def mxq(x, axis, fmt="e4m3"):
    dtype, down = {"e4m3": (ml_dtypes.float8_e4m3fn, 7), "e5m2": (ml_dtypes.float8_e5m2, 14)}[fmt]
    v = np.moveaxis(np.asarray(x, np.float32).astype(ml_dtypes.bfloat16).astype(np.float64), axis, -1)
    blocks = v.reshape(v.shape[:-1] + (-1, 32))
    amax = np.abs(blocks).max(-1, keepdims=True)
    byte = np.maximum(np.where(amax > 0, np.frexp(amax)[1] - 1 + 127, 0) - down, 1)
    scale = np.exp2(byte - 127.0)
    codes = (blocks / scale).astype(np.float32).astype(dtype).astype(np.float64)
    return np.moveaxis((codes * scale).reshape(v.shape), -1, axis)


WIDE = False


def mx_kscale(k):
    if not WIDE:
        return np.ones(k)
    levels = np.array([10, -10, 5, -5, 0])
    if k % 512:
        return np.exp2(np.random.permutation(np.resize(levels, k // 32))).repeat(32)
    a = np.empty((k // 512, 16))
    for p in range(k // 512):
        a[p, :8] = np.random.permutation(np.resize(levels, 8))
        for g in range(8):
            far = levels[np.abs(levels - a[p, g]) >= 10]
            a[p, g + 8] = far[np.random.randint(len(far))]
    return np.exp2(a.ravel()).repeat(32)


def f64(x):
    return np.asarray(x).astype(np.float64)


def striped(idx):
    return np.tile(idx.reshape(-1, 16).T, (8, 1)).astype(np.uint16)


def unstriped(offs):
    return offs[:16].T.reshape(-1).astype(np.int64)


E2M1 = np.array([0.0, 0.5, 1.0, 1.5, 2.0, 3.0, 4.0, 6.0, -0.0, -0.5, -1.0, -1.5, -2.0, -3.0, -4.0, -6.0])


def pack_weight(w, fmt):
    k, n = w.shape
    w = f64(np.asarray(w, np.float32).astype(ml_dtypes.bfloat16)).reshape(k // 32, 32, n)
    amax = np.abs(w).max(1)
    if fmt == "e4m3":
        byte = np.frexp(amax)[1] - 1 + 127 - 7
    else:
        mant, ex = np.frexp(amax / 6.0)
        byte = np.where(mant > 0.5, ex, ex - 1) + 127
    byte = np.clip(np.where(amax > 0, byte, 1), 1, 254)
    scaled = (w * np.exp2(127.0 - byte)[:, None, :]).reshape(k, n).astype(np.float32)
    by_word = np.ascontiguousarray(scaled.reshape(k // 512, 128, 4, n).transpose(0, 1, 3, 2))
    if fmt == "e4m3":
        words = by_word.astype(ml_dtypes.float8_e4m3fn).view(np.uint8)
    else:
        c = by_word.astype(ml_dtypes.float4_e2m1fn).view(np.uint8) & 0xF
        words = (c[..., 0::2] | (c[..., 1::2] << 4)).reshape(k // 512, 128, 2 * n)
    return np.ascontiguousarray(words), np.ascontiguousarray(byte.astype(np.uint8).reshape(k // 512, 16, n))


def unpack_weight(words, scales, fmt):
    g, _, n = scales.shape
    words = np.ascontiguousarray(words).reshape(g, 128, n, -1)
    if fmt == "e4m3":
        vals = words.view(ml_dtypes.float8_e4m3fn).astype(np.float64)
    else:
        nib = np.empty((g, 128, n, 4), np.uint8)
        nib[..., 0::2] = words & 0xF
        nib[..., 1::2] = words >> 4
        vals = E2M1[nib]
    vals = vals * np.repeat(np.exp2(scales.astype(np.float64) - 127.0), 8, axis=1)[..., None]
    return vals.transpose(0, 1, 3, 2).reshape(g * 512, n)


def gelu(v):
    return 0.5 * v * (1.0 + np.tanh(np.sqrt(2.0 / np.pi) * (v + 0.044715 * v**3)))


def bf(x):
    return np.asarray(x, np.float32).astype(ml_dtypes.bfloat16)


def planes(Y):
    n, m = Y.shape
    b = f64(bf(Y)).reshape(n // 32, 32, m)
    amax = np.abs(b).max(1)
    byte = np.clip(np.where(amax > 0, np.frexp(amax)[1] - 1 + 127 - 7, 1), 1, 254)
    codes = (b * np.exp2(127.0 - byte)[:, None, :]).reshape(n, m).astype(np.float32).astype(ml_dtypes.float8_e4m3fn).view(np.uint8)
    words = codes.reshape(n // 512, 128, 4, m).transpose(0, 1, 3, 2)
    return np.ascontiguousarray(words), np.ascontiguousarray(byte.astype(np.uint8).reshape(n // 512, 16, m))


K, T, S, H, P, N = 1024, 4096, 1024, 1024, 512, 512

def setup_inputs():
    n = np.random.standard_normal
    s = mx_kscale(K)[:, None]
    u = mx_kscale(H)
    size = np.exp(0.8 * n(N))
    perm = np.random.permutation(S)
    d = {}
    d["tab_words"], d["tab_scales"] = pack_weight(n((K, T)) * s, "e2m1")
    d["offs"] = striped(np.random.permutation(T)[:S])
    d["pos1"] = striped(perm[:P])
    d["pos2"] = striped(perm[P:2 * P])
    d["w1"] = (n((K, H)) / s / K ** 0.5).astype(np.float32)
    d["w2_words"], d["w2_scales"] = pack_weight(n((K, H)) / s / K ** 0.5, "e4m3")
    d["gain"] = (np.exp(0.3 * n(H)) * u).astype(np.float32)
    d["w3"] = (n((H, N)) / u[:, None] / H ** 0.5).astype(np.float32)
    d["b3"] = (0.5 * n(N)).astype(np.float32)
    d["depth"] = (1.5 * size * np.exp(0.2 * n(N))).astype(np.float32)
    d["w4_words"], d["w4_scales"] = pack_weight(0.8 * n((H, N)) * size / u[:, None] / H ** 0.5, "e2m1")
    return d

def reference(tab_words, tab_scales, offs, pos1, pos2, w1, w2_words, w2_scales, gain, w3, b3, depth, w4_words, w4_scales):
    v = unpack_weight(tab_words, tab_scales, "e2m1")[:, unstriped(offs)]
    w2 = unpack_weight(w2_words, w2_scales, "e4m3")
    w4 = unpack_weight(w4_words, w4_scales, "e2m1")
    left = mxq(f64(w1), 0, "e4m3").T @ v
    right = w2.T @ v
    h = np.maximum(left, right) * f64(gain)[:, None]
    wear = h[:, unstriped(pos1)] - h[:, unstriped(pos2)]
    wq = mxq(wear, 0, "e4m3")
    bounded = np.tanh((mxq(f64(w3), 0, "e4m3").T @ wq) + f64(b3)[:, None])
    direct = w4.T @ wq
    y = f64(depth)[:, None] * bounded + direct
    words, scales = planes(y)
    return y, words, scales

@@ -1,0 +1,351 @@
+from contextlib import ExitStack
+
+import concourse.mybir as mybir
+
+K, T, S, H, M, N = 1024, 4096, 1024, 1024, 512, 512
+FLOPS = 2 * (2 * K * H * S + 2 * H * N * M)
+
+F32 = mybir.dt.float32
+BF16 = mybir.dt.bfloat16
+I32 = mybir.dt.int32
+U32 = mybir.dt.uint32
+U16 = mybir.dt.uint16
+U8 = mybir.dt.uint8
+FP8X4 = mybir.dt.float8_e4m3fn_x4
+FP4X4 = mybir.dt.float4_e2m1fn_x4
+ALU = mybir.AluOpType
+ACT = mybir.ActivationFunctionType
+
+P = 128
+PACK = 4
+PASS = P * PACK
+BANK = 512
+
+
+def tile_list_worn_key_depths_kernel(
+    tc, tab_words, tab_scales, offs, pos1, pos2, w1, w2_words, w2_scales, gain, w3, b3, depth,
+    w4_words, w4_scales, out_0, out_1, out_2,
+):
+    nc = tc.nc
+    with ExitStack() as ctx:
+        lists = ctx.enter_context(tc.tile_pool(name="lists", bufs=1))
+        keep = ctx.enter_context(tc.tile_pool(name="keep", bufs=1))
+        ring = ctx.enter_context(tc.tile_pool(name="ring", bufs=4))
+        psum = ctx.enter_context(tc.psum_pool(name="psum", bufs=4))
+
+        def held(shape, dtype, name):
+            return keep.tile(shape, dtype, name=name, align_bytes=64)
+
+        def load_scale_rows(tile, scales, a_first):
+            for quad in range(4):
+                rows = scales[:, 4 * quad : 4 * quad + 4, :]
+                if a_first:
+                    nc.sync.dma_start(out=tile[32 * quad + 24 : 32 * quad + 32, :].bitcast(I32), in_=rows.bitcast(I32))
+                else:
+                    nc.sync.dma_start(
+                        out=tile[32 * quad : 32 * quad + 4, :, :].bitcast(I32),
+                        in_=rows.rearrange("a r c -> r a c").bitcast(I32),
+                    )
+
+        def load_weight(w, a, c0, c1, name):
+            raw = held([P, PACK, c1 - c0], F32, name)
+            nc.sync.dma_start(
+                out=raw[:], in_=w[PASS * a : PASS * (a + 1), c0:c1].rearrange("(p j) c -> p j c", j=PACK)
+            )
+            return raw
+
+        def round_weight(copy, raw, grouped, q0, q1, q_raw=0):
+            copy(
+                out=grouped[:].rearrange("p (t q j) -> p q t j", t=PACK, j=PACK)[:, q0:q1],
+                in_=raw[:].rearrange("p j (q t) -> p q t j", t=PACK)[:, q0 - q_raw : q1 - q_raw],
+            )
+
+        def quantize(grouped, name):
+            width = grouped.shape[1] // PACK
+            codes = held([P, width], U32, name + "_codes")
+            scales = held([P, width], U8, name + "_scales")
+            nc.vector.quantize_mx(out=codes[:].bitcast(FP8X4), scales=scales[:], in_=grouped)
+            return codes, scales
+
+        tab_scale_rows = held([P, T], U8, "tab_scale_rows")
+        for quad in range(4):
+            nc.vector.memset(tab_scale_rows[32 * quad : 32 * quad + 24, :].bitcast(I32), 0)
+        w2_scale_rows = held([P, 2, H], U8, "w2_scale_rows")
+        nc.gpsimd.memset(w2_scale_rows[:].bitcast(I32), 0)
+        v_scales = [held([P, S], U8, "v_scales0"), held([P, S], U8, "v_scales1")]
+        for a in range(2):
+            nc.gpsimd.memset(v_scales[a][:].bitcast(I32), 0)
+        w4_scale_rows = held([P, 2, N], U8, "w4_scale_rows")
+        nc.gpsimd.memset(w4_scale_rows[:].bitcast(I32), 0)
+
+        idx = lists.tile([P, S // 16], U16, name="idx")
+        nc.sync.dma_start(idx[:], offs)
+        load_scale_rows(tab_scale_rows, tab_scales, True)
+        tab = [held([P, T], U16, f"tab{a}") for a in range(2)]
+        for a in range(2):
+            nc.sync.dma_start(out=tab[a][:].bitcast(I32), in_=tab_words[a].bitcast(I32))
+        w1_raw = {(0, 0): load_weight(w1, 0, 0, PASS, "w1_raw00")}
+
+        def load_w2(b):
+            raw = held([P, 2, PASS], I32, f"w2_raw{b}")
+            nc.sync.dma_start(
+                out=raw[:],
+                in_=w2_words[:, :, PASS * b : PASS * (b + 1), :].rearrange("a p c i -> p a (c i)").bitcast(I32),
+            )
+            return raw
+
+        w2_raw = [load_w2(0)]
+        load_scale_rows(w2_scale_rows, w2_scales, False)
+        w1_last = [load_weight(w1, 1, 256 * u, 256 * (u + 1), f"w1_raw10{u}") for u in range(2)]
+        p2 = lists.tile([P, M // 16], U16, name="p2")
+        nc.sync.dma_start(p2[:], pos2)
+        p1 = lists.tile([P, M // 16], U16, name="p1")
+        nc.sync.dma_start(p1[:], pos1)
+        gains = held([P, 2, PACK], F32, "gains")
+        nc.sync.dma_start(out=gains[:], in_=gain.rearrange("(b p t) -> p b t", b=2, t=PACK))
+        w1_raw[0, 1] = load_weight(w1, 0, PASS, 2 * PASS, "w1_raw01")
+        w1_raw[1, 1] = load_weight(w1, 1, PASS, 2 * PASS, "w1_raw11")
+        w2_raw.append(load_w2(1))
+        w3_raw = [load_weight(w3, b, 0, N, f"w3_raw{b}") for b in range(2)]
+        w4_raw = held([P, 2, 2 * N], U8, "w4_raw")
+        nc.sync.dma_start(out=w4_raw[:].bitcast(I32), in_=w4_words.rearrange("a p c -> p a c").bitcast(I32))
+        load_scale_rows(w4_scale_rows, w4_scales, False)
+        biases = held([P, PACK], F32, "biases")
+        nc.sync.dma_start(out=biases[:], in_=b3.rearrange("(p t) -> p t", t=PACK))
+        depths = held([P, PACK], F32, "depths")
+        nc.sync.dma_start(out=depths[:], in_=depth.rearrange("(p t) -> p t", t=PACK))
+
+        warm = held([P, 2], F32, "warm")
+        nc.vector.memset(warm[:, 0:1], 0.0)
+        nc.scalar.activation(out=warm[:, 1:2], in_=warm[:, 0:1], func=ACT.Tanh)
+
+        v_words = [held([P, S], U16, f"v_words{a}") for a in range(2)]
+        picked_scale_rows = held([P, S], U8, "picked_scale_rows")
+        nc.vector.tensor_copy(picked_scale_rows[:], tab_scale_rows[:].indirect(idx[:]))
+        for a in range(2):
+            nc.scalar.dma_start(
+                out=v_scales[a][0:100, :].bitcast(I32), in_=picked_scale_rows[24 + 4 * a : 124 + 4 * a, :].bitcast(I32)
+            )
+        for a in range(2):
+            nc.vector.tensor_copy(v_words[a][:], tab[a][:].indirect(idx[:]))
+
+        w1_grouped = {key: ring.tile([P, PASS * PACK], BF16, name="grouped", bufs=3, align_bytes=64) for key in ((0, 0), (1, 0), (0, 1), (1, 1))}
+        w1_q = {}
+        w2_q = {}
+
+        def deal_w2(b):
+            words = held([P, 2, PASS], I32, f"w2_dealt{b}")
+            nc.vector.tensor_copy(
+                out=words[:].rearrange("p a (t g i) -> p a g t i", t=PACK, i=4),
+                in_=w2_raw[b][:].rearrange("p a (g i t) -> p a g t i", t=PACK, i=4),
+            )
+            scales = held([P, 2, PASS], U8, f"w2_dealt_scales{b}")
+            nc.vector.tensor_copy(
+                out=scales[:].rearrange("p a (t q) -> p a t q", t=PACK),
+                in_=w2_scale_rows[:, :, PASS * b : PASS * (b + 1)].rearrange("p a (q t) -> p a t q", t=PACK),
+            )
+            for a in range(2):
+                w2_q[a, b] = (words[:, a, :], scales[:, a, :])
+
+        round_weight(nc.scalar.copy, w1_raw[0, 0], w1_grouped[0, 0], 0, P)
+        deal_w2(0)
+        w1_q[0, 0] = quantize(w1_grouped[0, 0][:], "w1_00")
+        round_weight(nc.scalar.copy, w1_last[0], w1_grouped[1, 0], 0, P // 2)
+        round_weight(nc.vector.tensor_copy, w1_last[1], w1_grouped[1, 0], P // 2, P, P // 2)
+        w1_q[1, 0] = quantize(w1_grouped[1, 0][:], "w1_10")
+
+        w3_grouped = [ring.tile([P, PASS * PACK], BF16, name="grouped", bufs=3, align_bytes=64) for b in range(2)]
+        w3_q = {}
+        w4_q = {}
+
+        def deal_w4():
+            words = held([P, 2, 2 * N], U8, "w4_dealt")
+            nc.vector.tensor_copy(
+                out=words[:].bitcast(U16).rearrange("p a (t q) -> p a t q", t=PACK),
+                in_=w4_raw[:].bitcast(U16).rearrange("p a (q t) -> p a t q", t=PACK),
+            )
+            scales = held([P, 2, N], U8, "w4_dealt_scales")
+            nc.vector.tensor_copy(
+                out=scales[:].rearrange("p a (t q) -> p a t q", t=PACK),
+                in_=w4_scale_rows[:].rearrange("p a (q t) -> p a t q", t=PACK),
+            )
+            for b in range(2):
+                w4_q[b] = (words[:, b, :], scales[:, b, :])
+
+        stronger = [held([P, S], F32, f"stronger{i}") for i in range(8)]
+        wear_rows = [held([P, PACK, M], BF16, f"wear_rows{b}") for b in range(2)]
+        wear_grouped = [held([P, M * PACK], BF16, f"wear_grouped{b}") for b in range(2)]
+        wear_codes = [held([P, M], U32, f"wear_codes{b}") for b in range(2)]
+        wear_scales = [held([P, M], U8, f"wear_scales{b}") for b in range(2)]
+
+        right_copy = {}
+
+        def first_stage(i):
+            b, t = divmod(i, PACK)
+            rows = slice(P * t, P * (t + 1))
+            right_copy[i] = ring.tile([P, S], F32, name="right_copy", bufs=4)
+            bank = {}
+            for name, weight in (("right", w2_q), ("left", w1_q)):
+                for half in range(2):
+                    cols = slice(BANK * half, BANK * (half + 1))
+                    bank[name, half] = psum.tile([P, BANK], F32, name=name, tag=name)
+                    for a in range(2):
+                        codes, scales = weight[a, b]
+                        nc.tensor.matmul_mx(
+                            out=bank[name, half][:], lhsT=codes[:, rows].bitcast(FP8X4), lhsT_scale=scales[:, rows],
+                            rhs=v_words[a][:, cols].bitcast(FP4X4), rhs_scale=v_scales[a][:, cols],
+                            start=(a == 0), stop=(a == 1),
+                        )
+                    if name == "right":
+                        nc.scalar.copy(out=right_copy[i][:, cols], in_=bank[name, half][:])
+                    else:
+                        nc.vector.tensor_tensor(stronger[i][:, cols], bank[name, half][:], right_copy[i][:, cols], ALU.max)
+
+        picked = {}
+
+        def pick_catalogue(i, m0, m1, place):
+            nc.vector.tensor_copy(place, stronger[i][:].indirect(p2[:, m0 // 16 : m1 // 16]))
+            picked[i, m0] = place
+
+        def pick_worn(i, m0, m1, place):
+            b, t = divmod(i, PACK)
+            nc.vector.tensor_tensor(place, stronger[i][:].indirect(p1[:, m0 // 16 : m1 // 16]), picked[i, m0], ALU.subtract)
+            nc.scalar.activation(out=wear_rows[b][:, t, m0:m1], in_=place, func=ACT.Copy, scale=gains[:, b, t : t + 1])
+
+        def group_wear(b, m0, m1):
+            nc.scalar.copy(
+                out=wear_grouped[b][:, PACK * m0 : PACK * m1].rearrange("p (g i t) -> p g t i", t=PACK, i=4),
+                in_=wear_rows[b][:, :, m0:m1].rearrange("p t (g i) -> p g t i", i=4),
+            )
+
+        def quantize_wear(b, m0, m1):
+            nc.vector.quantize_mx(
+                out=wear_codes[b][:, m0:m1].bitcast(FP8X4), scales=wear_scales[b][:, m0:m1],
+                in_=wear_grouped[b][:, PACK * m0 : PACK * m1],
+            )
+
+        catalogue_at = {1: 0, 2: 1, 4: 2, 5: 3}
+        worn_at = {2: 0, 3: 1, 5: 2, 6: 3}
+        for i in range(8):
+            first_stage(i)
+            free = [right_copy[i][:, 0:BANK], right_copy[i][:, BANK:S]]
+            if i in catalogue_at:
+                pick_catalogue(catalogue_at[i], 0, M, free.pop(0))
+            if i in worn_at:
+                pick_worn(worn_at[i], 0, M, free.pop(0))
+            if i < 2:
+                round_weight(nc.scalar.copy, w1_raw[i, 1], w1_grouped[i, 1], 0, P // 2)
+                round_weight(nc.scalar.copy, w1_raw[i, 1], w1_grouped[i, 1], P // 2, P)
+            if i in (1, 2):
+                w1_q[i - 1, 1] = quantize(w1_grouped[i - 1, 1][:], f"w1_{i - 1}1")
+            if i == 2:
+                deal_w2(1)
+            if 3 <= i < 7:
+                b, part = divmod(i - 3, 2)
+                round_weight(nc.scalar.copy, w3_raw[b], w3_grouped[b], part * P // 2, (part + 1) * P // 2)
+            if i == 4:
+                deal_w4()
+            if i == 5:
+                w3_q[0] = quantize(w3_grouped[0][:], "w3_0")
+            if i == 6:
+                group_wear(0, 0, M)
+            if i == 7:
+                w3_q[1] = quantize(w3_grouped[1][:], "w3_1")
+                quantize_wear(0, 0, M)
+
+        chunks = [(0, 256), (256, 384), (384, 512)]
+        banks = {}
+
+        def second_stage(c, b):
+            m0, m1 = chunks[c]
+            width = m1 - m0
+            per_bank = BANK // width
+            for first in range(0, PACK, per_bank):
+                if b == 0:
+                    bounded = psum.tile([P, per_bank, width], F32, name="bounded", tag="right")
+                    direct = psum.tile([P, per_bank, width], F32, name="direct", tag="left")
+                    for u in range(per_bank):
+                        banks[c, first + u] = (bounded[:, u, :], direct[:, u, :])
+                for t in range(first, first + per_bank):
+                    rows = slice(P * t, P * (t + 1))
+                    codes, scales = w3_q[b]
+                    nc.tensor.matmul_mx(
+                        out=banks[c, t][0], lhsT=codes[:, rows].bitcast(FP8X4), lhsT_scale=scales[:, rows],
+                        rhs=wear_codes[b][:, m0:m1].bitcast(FP8X4), rhs_scale=wear_scales[b][:, m0:m1],
+                        start=(b == 0 and t == first), stop=(b == 1 and t == first + per_bank - 1),
+                    )
+                for t in range(first, first + per_bank):
+                    rows = slice(P * t, P * (t + 1))
+                    words, scales = w4_q[b]
+                    for s in range(0, width, P):
+                        cols = slice(m0 + s, m0 + s + P)
+                        nc.tensor.matmul_mx(
+                            out=banks[c, t][1][:, s : s + P],
+                            lhsT=words[:, 2 * P * t : 2 * P * (t + 1)].bitcast(FP4X4), lhsT_scale=scales[:, rows],
+                            rhs=wear_codes[b][:, cols].bitcast(FP8X4), rhs_scale=wear_scales[b][:, cols],
+                            start=(b == 0 and t == first and s == 0),
+                            stop=(b == 1 and t == first + per_bank - 1 and s == width - P),
+                        )
+
+        y_codes = held([P, M], U32, "y_codes")
+        y_scales = held([P, M], U8, "y_scales")
+        y_rows = out_0.rearrange("(p t) m -> p t m", t=PACK)
+        y = [held([P, PACK, m1 - m0], F32, f"y{m0}") for m0, m1 in chunks]
+        y_grouped = [held([P, (m1 - m0) * PACK], BF16, f"y_grouped{m0}") for m0, m1 in chunks]
+
+        def finish(c, copy):
+            m0, m1 = chunks[c]
+            for t in range(PACK):
+                bounded, direct = banks[c, t]
+                squashed = ring.tile([P, m1 - m0], F32, name="squashed")
+                nc.scalar.activation(out=squashed[:], in_=bounded, func=ACT.Tanh, bias=biases[:, t : t + 1])
+                nc.vector.scalar_tensor_tensor(y[c][:, t, :], squashed[:], depths[:, t : t + 1], direct, ALU.mult, ALU.add)
+            nc.sync.dma_start(out=y_rows[:, :, m0:m1], in_=y[c][:])
+            copy(
+                out=y_grouped[c][:].rearrange("p (g i t) -> p g t i", t=PACK, i=4),
+                in_=y[c][:].rearrange("p t (g i) -> p g t i", i=4),
+            )
+
+        def planes(c):
+            m0, m1 = chunks[c]
+            nc.vector.quantize_mx(out=y_codes[:, m0:m1].bitcast(FP8X4), scales=y_scales[:, m0:m1], in_=y_grouped[c][:])
+            nc.sync.dma_start(
+                out=out_1[0].rearrange("p m t -> p (m t)")[:, PACK * m0 : PACK * m1].bitcast(I32),
+                in_=y_codes[:, m0:m1].bitcast(I32),
+            )
+
+        def pick_chunk(c, room):
+            m0, m1 = chunks[c]
+            width = m1 - m0
+            for t in range(PACK + 1):
+                if t < PACK:
+                    pick_catalogue(PACK + t, m0, m1, room(t))
+                if t > 0:
+                    diff = ring.tile([P, width], F32, name="diff")
+                    pick_worn(PACK + t - 1, m0, m1, diff[:])
+            group_wear(1, m0, m1)
+
+        for c in range(3):
+            second_stage(c, 0)
+        pick_chunk(0, lambda t: right_copy[7][:, 256 * t : 256 * (t + 1)])
+        pick_chunk(1, lambda t: right_copy[7][:, 256 * t : 256 * t + P])
+        quantize_wear(1, *chunks[0])
+        second_stage(0, 1)
+        freed = wear_grouped[1][:, 0 : PACK * 256].bitcast(F32)
+        pick_chunk(2, lambda t: freed[:, P * t : P * (t + 1)])
+        quantize_wear(1, *chunks[1])
+        second_stage(1, 1)
+        finish(0, nc.scalar.copy)
+        quantize_wear(1, *chunks[2])
+        second_stage(2, 1)
+        finish(1, nc.scalar.copy)
+        planes(0)
+        finish(2, nc.vector.tensor_copy)
+        planes(1)
+        planes(2)
+        for quad in range(4):
+            queue = nc.sync if quad % 2 == 0 else nc.scalar
+            queue.dma_start(
+                out=out_2[0, 4 * quad : 4 * quad + 4, :].bitcast(I32),
+                in_=y_scales[32 * quad : 32 * quad + 4, :].bitcast(I32),
+            )

@@ -36,19 +36,22 @@ def tile_list_worn_key_depths_kernel(
         def held(shape, dtype, name):
             return keep.tile(shape, dtype, name=name, align_bytes=64)
 
-        def load_scale_rows(tile, scales, a_first):
+        def staged(shape, dtype, name, room):
+            return keep.tile(shape, dtype, name=name, tag=room, align_bytes=64)
+
+        def load_scale_rows(queue, tile, scales, a_first):
             for quad in range(4):
                 rows = scales[:, 4 * quad : 4 * quad + 4, :]
                 if a_first:
                     nc.sync.dma_start(out=tile[32 * quad + 24 : 32 * quad + 32, :].bitcast(I32), in_=rows.bitcast(I32))
                 else:
-                    nc.sync.dma_start(
+                    queue.dma_start(
                         out=tile[32 * quad : 32 * quad + 4, :, :].bitcast(I32),
                         in_=rows.rearrange("a r c -> r a c").bitcast(I32),
                     )
 
-        def load_weight(w, a, c0, c1, name):
-            raw = held([P, PACK, c1 - c0], F32, name)
+        def load_weight(w, a, c0, c1, room):
+            raw = staged([P, PACK, c1 - c0], F32, "raw", room)
             nc.sync.dma_start(
                 out=raw[:], in_=w[PASS * a : PASS * (a + 1), c0:c1].rearrange("(p j) c -> p j c", j=PACK)
             )
@@ -56,18 +59,25 @@ def tile_list_worn_key_depths_kernel(
 
         def round_weight(copy, raw, grouped, q0, q1, q_raw=0):
             copy(
-                out=grouped[:].rearrange("p (t q j) -> p q t j", t=PACK, j=PACK)[:, q0:q1],
+                out=grouped.rearrange("p (t q j) -> p q t j", t=PACK, j=PACK)[:, q0:q1],
                 in_=raw[:].rearrange("p j (q t) -> p q t j", t=PACK)[:, q0 - q_raw : q1 - q_raw],
             )
 
-        def quantize(grouped, name):
-            width = grouped.shape[1] // PACK
-            codes = held([P, width], U32, name + "_codes")
-            scales = held([P, width], U8, name + "_scales")
-            nc.vector.quantize_mx(out=codes[:].bitcast(FP8X4), scales=scales[:], in_=grouped)
-            return codes, scales
+        def quantize_part(operand, grouped, c0, c1):
+            codes, scales = operand
+            nc.vector.quantize_mx(
+                out=codes[:, c0:c1].bitcast(FP8X4), scales=scales[:, c0:c1], in_=grouped[:, PACK * c0 : PACK * c1]
+            )
 
-        tab_scale_rows = held([P, T], U8, "tab_scale_rows")
+        def operand_tiles(name):
+            return held([P, PASS], U32, name + "_codes"), held([P, PASS], U8, name + "_scales")
+
+        def quantize(grouped, name):
+            operand = operand_tiles(name)
+            quantize_part(operand, grouped, 0, PASS)
+            return operand
+
+        tab_scale_rows = staged([P, T], U8, "tab_scale_rows", "room_c")
         for quad in range(4):
             nc.vector.memset(tab_scale_rows[32 * quad : 32 * quad + 24, :].bitcast(I32), 0)
         w2_scale_rows = held([P, 2, H], U8, "w2_scale_rows")
@@ -75,66 +85,56 @@ def tile_list_worn_key_depths_kernel(
         v_scales = [held([P, S], U8, "v_scales0"), held([P, S], U8, "v_scales1")]
         for a in range(2):
             nc.gpsimd.memset(v_scales[a][:].bitcast(I32), 0)
-        w4_scale_rows = held([P, 2, N], U8, "w4_scale_rows")
-        nc.gpsimd.memset(w4_scale_rows[:].bitcast(I32), 0)
 
         idx = lists.tile([P, S // 16], U16, name="idx")
         nc.sync.dma_start(idx[:], offs)
-        load_scale_rows(tab_scale_rows, tab_scales, True)
-        tab = [held([P, T], U16, f"tab{a}") for a in range(2)]
+        load_scale_rows(nc.sync, tab_scale_rows, tab_scales, True)
+        picked_scale_rows = staged([P, S], U8, "picked_scale_rows", "room_f")
+        nc.vector.tensor_copy(picked_scale_rows[:], tab_scale_rows[:].indirect(idx[:]))
+        for a in range(2):
+            nc.scalar.dma_start(
+                out=v_scales[a][0:100, :].bitcast(I32), in_=picked_scale_rows[24 + 4 * a : 124 + 4 * a, :].bitcast(I32)
+            )
+        tab = [staged([P, T], U16, f"tab{a}", ("room_a", "room_b")[a]) for a in range(2)]
         for a in range(2):
             nc.sync.dma_start(out=tab[a][:].bitcast(I32), in_=tab_words[a].bitcast(I32))
-        w1_raw = {(0, 0): load_weight(w1, 0, 0, PASS, "w1_raw00")}
 
-        def load_w2(b):
-            raw = held([P, 2, PASS], I32, f"w2_raw{b}")
+        def load_w2(b, room):
+            raw = staged([P, 2, PASS], I32, f"w2_raw{b}", room)
             nc.sync.dma_start(
                 out=raw[:],
                 in_=w2_words[:, :, PASS * b : PASS * (b + 1), :].rearrange("a p c i -> p a (c i)").bitcast(I32),
             )
             return raw
 
-        w2_raw = [load_w2(0)]
-        load_scale_rows(w2_scale_rows, w2_scales, False)
-        w1_last = [load_weight(w1, 1, 256 * u, 256 * (u + 1), f"w1_raw10{u}") for u in range(2)]
+        w1_raw = {(0, 0): load_weight(w1, 0, 0, PASS, "room_d")}
+        load_scale_rows(nc.sync, w2_scale_rows, w2_scales, False)
+        w2_raw = [load_w2(0, "room_e")]
+        w1_last = [load_weight(w1, 1, 256 * u, 256 * (u + 1), f"w1_last{u}") for u in range(2)]
         p2 = lists.tile([P, M // 16], U16, name="p2")
         nc.sync.dma_start(p2[:], pos2)
         p1 = lists.tile([P, M // 16], U16, name="p1")
         nc.sync.dma_start(p1[:], pos1)
-        gains = held([P, 2, PACK], F32, "gains")
-        nc.sync.dma_start(out=gains[:], in_=gain.rearrange("(b p t) -> p b t", b=2, t=PACK))
-        w1_raw[0, 1] = load_weight(w1, 0, PASS, 2 * PASS, "w1_raw01")
-        w1_raw[1, 1] = load_weight(w1, 1, PASS, 2 * PASS, "w1_raw11")
-        w2_raw.append(load_w2(1))
-        w3_raw = [load_weight(w3, b, 0, N, f"w3_raw{b}") for b in range(2)]
-        w4_raw = held([P, 2, 2 * N], U8, "w4_raw")
-        nc.sync.dma_start(out=w4_raw[:].bitcast(I32), in_=w4_words.rearrange("a p c -> p a c").bitcast(I32))
-        load_scale_rows(w4_scale_rows, w4_scales, False)
-        biases = held([P, PACK], F32, "biases")
-        nc.sync.dma_start(out=biases[:], in_=b3.rearrange("(p t) -> p t", t=PACK))
-        depths = held([P, PACK], F32, "depths")
-        nc.sync.dma_start(out=depths[:], in_=depth.rearrange("(p t) -> p t", t=PACK))
 
         warm = held([P, 2], F32, "warm")
         nc.vector.memset(warm[:, 0:1], 0.0)
         nc.scalar.activation(out=warm[:, 1:2], in_=warm[:, 0:1], func=ACT.Tanh)
 
         v_words = [held([P, S], U16, f"v_words{a}") for a in range(2)]
-        picked_scale_rows = held([P, S], U8, "picked_scale_rows")
-        nc.vector.tensor_copy(picked_scale_rows[:], tab_scale_rows[:].indirect(idx[:]))
-        for a in range(2):
-            nc.scalar.dma_start(
-                out=v_scales[a][0:100, :].bitcast(I32), in_=picked_scale_rows[24 + 4 * a : 124 + 4 * a, :].bitcast(I32)
-            )
         for a in range(2):
             nc.vector.tensor_copy(v_words[a][:], tab[a][:].indirect(idx[:]))
+        w1_raw[0, 1] = load_weight(w1, 0, PASS, 2 * PASS, "room_a")
+        w1_raw[1, 1] = load_weight(w1, 1, PASS, 2 * PASS, "room_b")
+        w2_raw.append(load_w2(1, "room_c"))
+        gains = staged([P, 2, PACK], F32, "gains", "room_f")
+        nc.sync.dma_start(out=gains[:], in_=gain.rearrange("(b p t) -> p b t", b=2, t=PACK))
 
-        w1_grouped = {key: ring.tile([P, PASS * PACK], BF16, name="grouped", bufs=3, align_bytes=64) for key in ((0, 0), (1, 0), (0, 1), (1, 1))}
+        w1_grouped = {(a, 0): staged([P, PASS * PACK], BF16, "grouped", f"grouped{a}") for a in range(2)}
         w1_q = {}
         w2_q = {}
 
         def deal_w2(b):
-            words = held([P, 2, PASS], I32, f"w2_dealt{b}")
+            words = staged([P, 2, PASS], I32, f"w2_dealt{b}", ("w2_dealt", "grouped0")[b])
             nc.vector.tensor_copy(
                 out=words[:].rearrange("p a (t g i) -> p a g t i", t=PACK, i=4),
                 in_=w2_raw[b][:].rearrange("p a (g i t) -> p a g t i", t=PACK, i=4),
@@ -147,24 +147,36 @@ def tile_list_worn_key_depths_kernel(
             for a in range(2):
                 w2_q[a, b] = (words[:, a, :], scales[:, a, :])
 
-        round_weight(nc.scalar.copy, w1_raw[0, 0], w1_grouped[0, 0], 0, P)
         deal_w2(0)
-        w1_q[0, 0] = quantize(w1_grouped[0, 0][:], "w1_00")
-        round_weight(nc.scalar.copy, w1_last[0], w1_grouped[1, 0], 0, P // 2)
-        round_weight(nc.vector.tensor_copy, w1_last[1], w1_grouped[1, 0], P // 2, P, P // 2)
-        w1_q[1, 0] = quantize(w1_grouped[1, 0][:], "w1_10")
+        round_weight(nc.scalar.copy, w1_raw[0, 0], w1_grouped[0, 0][:], 0, P)
+        round_weight(nc.scalar.copy, w1_last[0], w1_grouped[1, 0][:], 0, P // 2)
+        round_weight(nc.vector.tensor_copy, w1_last[1], w1_grouped[1, 0][:], P // 2, P, P // 2)
+        for a in range(2):
+            w1_q[a, 0] = operand_tiles(f"w1_{a}0")
+        for c0 in (0, PASS // 2):
+            for a in range(2):
+                quantize_part(w1_q[a, 0], w1_grouped[a, 0][:], c0, c0 + PASS // 2)
 
-        w3_grouped = [ring.tile([P, PASS * PACK], BF16, name="grouped", bufs=3, align_bytes=64) for b in range(2)]
+        w3_raw = [load_weight(w3, 0, 0, N, "room_d")]
+        w4_raw = staged([P, 2, 2 * N], U8, "w4_raw", "room_e")
+        nc.sync.dma_start(out=w4_raw[:].bitcast(I32), in_=w4_words.rearrange("a p c -> p a c").bitcast(I32))
+        w4_scale_rows = staged([P, 2, N], U8, "w4_scale_rows", "w1_last0")
+        nc.gpsimd.memset(w4_scale_rows[:].bitcast(I32), 0)
+        load_scale_rows(nc.sync, w4_scale_rows, w4_scales, False)
+        biases = staged([P, PACK], F32, "biases", "w1_last1")
+        nc.sync.dma_start(out=biases[:], in_=b3.rearrange("(p t) -> p t", t=PACK))
+        depths = staged([P, PACK], F32, "depths", "grouped1")
+        nc.sync.dma_start(out=depths[:], in_=depth.rearrange("(p t) -> p t", t=PACK))
         w3_q = {}
         w4_q = {}
 
         def deal_w4():
-            words = held([P, 2, 2 * N], U8, "w4_dealt")
+            words = staged([P, 2, 2 * N], U8, "w4_dealt", "right41")
             nc.vector.tensor_copy(
                 out=words[:].bitcast(U16).rearrange("p a (t q) -> p a t q", t=PACK),
                 in_=w4_raw[:].bitcast(U16).rearrange("p a (q t) -> p a t q", t=PACK),
             )
-            scales = held([P, 2, N], U8, "w4_dealt_scales")
+            scales = staged([P, 2, N], U8, "w4_dealt_scales", "right1")
             nc.vector.tensor_copy(
                 out=scales[:].rearrange("p a (t q) -> p a t q", t=PACK),
                 in_=w4_scale_rows[:].rearrange("p a (q t) -> p a t q", t=PACK),
@@ -178,28 +190,36 @@ def tile_list_worn_key_depths_kernel(
         wear_codes = [held([P, M], U32, f"wear_codes{b}") for b in range(2)]
         wear_scales = [held([P, M], U8, f"wear_scales{b}") for b in range(2)]
 
+        halves = [slice(0, BANK), slice(BANK, S)]
         right_copy = {}
 
-        def first_stage(i):
+        def product(i, weight, name):
             b, t = divmod(i, PACK)
             rows = slice(P * t, P * (t + 1))
-            right_copy[i] = ring.tile([P, S], F32, name="right_copy", bufs=4)
-            bank = {}
-            for name, weight in (("right", w2_q), ("left", w1_q)):
-                for half in range(2):
-                    cols = slice(BANK * half, BANK * (half + 1))
-                    bank[name, half] = psum.tile([P, BANK], F32, name=name, tag=name)
-                    for a in range(2):
-                        codes, scales = weight[a, b]
-                        nc.tensor.matmul_mx(
-                            out=bank[name, half][:], lhsT=codes[:, rows].bitcast(FP8X4), lhsT_scale=scales[:, rows],
-                            rhs=v_words[a][:, cols].bitcast(FP4X4), rhs_scale=v_scales[a][:, cols],
-                            start=(a == 0), stop=(a == 1),
-                        )
-                    if name == "right":
-                        nc.scalar.copy(out=right_copy[i][:, cols], in_=bank[name, half][:])
-                    else:
-                        nc.vector.tensor_tensor(stronger[i][:, cols], bank[name, half][:], right_copy[i][:, cols], ALU.max)
+            bank = [psum.tile([P, BANK], F32, name=name, tag=name) for cols in halves]
+            for a in range(2):
+                codes, scales = weight[a, b]
+                for half, cols in enumerate(halves):
+                    nc.tensor.matmul_mx(
+                        out=bank[half][:], lhsT=codes[:, rows].bitcast(FP8X4), lhsT_scale=scales[:, rows],
+                        rhs=v_words[a][:, cols].bitcast(FP4X4), rhs_scale=v_scales[a][:, cols],
+                        start=(a == 0), stop=(a == 1),
+                    )
+            return bank
+
+        def right_reading(i):
+            if i == 4:
+                parts = [staged([P, BANK], F32, "right_half", f"right4{half}") for half in range(2)]
+                right_copy[i] = [part[:] for part in parts]
+            else:
+                whole = staged([P, S], F32, "right_copy", f"right{i}")
+                right_copy[i] = [whole[:, cols] for cols in halves] + [whole[:]]
+            for half, bank in enumerate(product(i, w2_q, "right")):
+                nc.scalar.copy(out=right_copy[i][half], in_=bank[:])
+
+        def left_reading(i):
+            for half, bank in enumerate(product(i, w1_q, "left")):
+                nc.vector.tensor_tensor(stronger[i][:, halves[half]], bank[:], right_copy[i][half], ALU.max)
 
         picked = {}
 
@@ -224,34 +244,49 @@ def tile_list_worn_key_depths_kernel(
                 in_=wear_grouped[b][:, PACK * m0 : PACK * m1],
             )
 
-        catalogue_at = {1: 0, 2: 1, 4: 2, 5: 3}
-        worn_at = {2: 0, 3: 1, 5: 2, 6: 3}
-        for i in range(8):
-            first_stage(i)
-            free = [right_copy[i][:, 0:BANK], right_copy[i][:, BANK:S]]
-            if i in catalogue_at:
-                pick_catalogue(catalogue_at[i], 0, M, free.pop(0))
-            if i in worn_at:
-                pick_worn(worn_at[i], 0, M, free.pop(0))
-            if i < 2:
-                round_weight(nc.scalar.copy, w1_raw[i, 1], w1_grouped[i, 1], 0, P // 2)
-                round_weight(nc.scalar.copy, w1_raw[i, 1], w1_grouped[i, 1], P // 2, P)
-            if i in (1, 2):
-                w1_q[i - 1, 1] = quantize(w1_grouped[i - 1, 1][:], f"w1_{i - 1}1")
-            if i == 2:
-                deal_w2(1)
-            if 3 <= i < 7:
-                b, part = divmod(i - 3, 2)
-                round_weight(nc.scalar.copy, w3_raw[b], w3_grouped[b], part * P // 2, (part + 1) * P // 2)
-            if i == 4:
-                deal_w4()
-            if i == 5:
-                w3_q[0] = quantize(w3_grouped[0][:], "w3_0")
-            if i == 6:
-                group_wear(0, 0, M)
-            if i == 7:
-                w3_q[1] = quantize(w3_grouped[1][:], "w3_1")
-                quantize_wear(0, 0, M)
+        def round_late(raw, i):
+            grouped = right_copy[i][2].bitcast(BF16)
+            for q0 in range(0, P, P // 4):
+                round_weight(nc.scalar.copy, raw, grouped, q0, q0 + P // 4)
+            return grouped
+
+        right_reading(0)
+        left_reading(0)
+        right_reading(1)
+        pick_catalogue(0, 0, M, held([P, M], F32, "catalogue0")[:])
+        left_reading(1)
+        right_reading(2)
+        right_reading(3)
+        deal_w2(1)
+        grouped01 = round_late(w1_raw[0, 1], 0)
+        w3_raw.append(load_weight(w3, 1, 0, N, "room_a"))
+        left_reading(2)
+        right_reading(4)
+        pick_catalogue(1, 0, M, right_copy[2][0])
+        pick_worn(0, 0, M, right_copy[2][1])
+        grouped11 = round_late(w1_raw[1, 1], 1)
+        w1_q[0, 1] = quantize(grouped01, "w1_01")
+        left_reading(3)
+        right_reading(5)
+        pick_worn(1, 0, M, held([P, M], F32, "diff1")[:])
+        w1_q[1, 1] = quantize(grouped11, "w1_11")
+        left_reading(4)
+        right_reading(6)
+        pick_catalogue(2, 0, M, right_copy[4][0])
+        w3_early = round_late(w3_raw[0], 3)
+        left_reading(5)
+        right_reading(7)
+        pick_catalogue(3, 0, M, right_copy[5][0])
+        pick_worn(2, 0, M, right_copy[5][1])
+        deal_w4()
+        w3_late = round_late(w3_raw[1], 0)
+        left_reading(6)
+        pick_worn(3, 0, M, right_copy[6][0])
+        w3_q[0] = quantize(w3_early, "w3_0")
+        group_wear(0, 0, M)
+        left_reading(7)
+        w3_q[1] = quantize(w3_late, "w3_1")
+        quantize_wear(0, 0, M)
 
         chunks = [(0, 256), (256, 384), (384, 512)]
         banks = {}
@@ -327,18 +362,18 @@ def tile_list_worn_key_depths_kernel(
 
         for c in range(3):
             second_stage(c, 0)
-        pick_chunk(0, lambda t: right_copy[7][:, 256 * t : 256 * (t + 1)])
-        pick_chunk(1, lambda t: right_copy[7][:, 256 * t : 256 * t + P])
+        pick_chunk(0, lambda t: right_copy[7][2][:, 256 * t : 256 * (t + 1)])
+        pick_chunk(1, lambda t: right_copy[7][2][:, 256 * t : 256 * t + P])
         quantize_wear(1, *chunks[0])
         second_stage(0, 1)
         freed = wear_grouped[1][:, 0 : PACK * 256].bitcast(F32)
         pick_chunk(2, lambda t: freed[:, P * t : P * (t + 1)])
         quantize_wear(1, *chunks[1])
         second_stage(1, 1)
-        finish(0, nc.scalar.copy)
+        finish(0, nc.vector.tensor_copy)
         quantize_wear(1, *chunks[2])
         second_stage(2, 1)
-        finish(1, nc.scalar.copy)
+        finish(1, nc.vector.tensor_copy)
         planes(0)
         finish(2, nc.vector.tensor_copy)
         planes(1)

from contextlib import ExitStack

import concourse.mybir as mybir

K, T, S, H, M, N = 1024, 4096, 1024, 1024, 512, 512
FLOPS = 2 * (2 * K * H * S + 2 * H * N * M)

F32 = mybir.dt.float32
BF16 = mybir.dt.bfloat16
I32 = mybir.dt.int32
U32 = mybir.dt.uint32
U16 = mybir.dt.uint16
U8 = mybir.dt.uint8
FP8X4 = mybir.dt.float8_e4m3fn_x4
FP4X4 = mybir.dt.float4_e2m1fn_x4
ALU = mybir.AluOpType
ACT = mybir.ActivationFunctionType

P = 128
PACK = 4
PASS = P * PACK
BANK = 512


def tile_list_worn_key_depths_kernel(
    tc, tab_words, tab_scales, offs, pos1, pos2, w1, w2_words, w2_scales, gain, w3, b3, depth,
    w4_words, w4_scales, out_0, out_1, out_2,
):
    nc = tc.nc
    with ExitStack() as ctx:
        lists = ctx.enter_context(tc.tile_pool(name="lists", bufs=1))
        keep = ctx.enter_context(tc.tile_pool(name="keep", bufs=1))
        ring = ctx.enter_context(tc.tile_pool(name="ring", bufs=4))
        psum = ctx.enter_context(tc.psum_pool(name="psum", bufs=4))

        def held(shape, dtype, name):
            return keep.tile(shape, dtype, name=name, align_bytes=64)

        def staged(shape, dtype, name, room):
            return keep.tile(shape, dtype, name=name, tag=room, align_bytes=64)

        def load_scale_rows(queue, tile, scales, a_first):
            for quad in range(4):
                rows = scales[:, 4 * quad : 4 * quad + 4, :]
                if a_first:
                    nc.sync.dma_start(out=tile[32 * quad + 24 : 32 * quad + 32, :].bitcast(I32), in_=rows.bitcast(I32))
                else:
                    queue.dma_start(
                        out=tile[32 * quad : 32 * quad + 4, :, :].bitcast(I32),
                        in_=rows.rearrange("a r c -> r a c").bitcast(I32),
                    )

        def load_weight(w, a, c0, c1, room):
            raw = staged([P, PACK, c1 - c0], F32, "raw", room)
            nc.sync.dma_start(
                out=raw[:], in_=w[PASS * a : PASS * (a + 1), c0:c1].rearrange("(p j) c -> p j c", j=PACK)
            )
            return raw

        def round_weight(copy, raw, grouped, q0, q1, q_raw=0):
            copy(
                out=grouped.rearrange("p (t q j) -> p q t j", t=PACK, j=PACK)[:, q0:q1],
                in_=raw[:].rearrange("p j (q t) -> p q t j", t=PACK)[:, q0 - q_raw : q1 - q_raw],
            )

        def quantize_part(operand, grouped, c0, c1):
            codes, scales = operand
            nc.vector.quantize_mx(
                out=codes[:, c0:c1].bitcast(FP8X4), scales=scales[:, c0:c1], in_=grouped[:, PACK * c0 : PACK * c1]
            )

        def operand_tiles(name):
            return held([P, PASS], U32, name + "_codes"), held([P, PASS], U8, name + "_scales")

        def quantize(grouped, name):
            operand = operand_tiles(name)
            quantize_part(operand, grouped, 0, PASS)
            return operand

        tab_scale_rows = staged([P, T], U8, "tab_scale_rows", "room_c")
        for quad in range(4):
            nc.vector.memset(tab_scale_rows[32 * quad : 32 * quad + 24, :].bitcast(I32), 0)
        w2_scale_rows = held([P, 2, H], U8, "w2_scale_rows")
        nc.gpsimd.memset(w2_scale_rows[:].bitcast(I32), 0)
        v_scales = [held([P, S], U8, "v_scales0"), held([P, S], U8, "v_scales1")]
        for a in range(2):
            nc.gpsimd.memset(v_scales[a][:].bitcast(I32), 0)

        idx = lists.tile([P, S // 16], U16, name="idx")
        nc.sync.dma_start(idx[:], offs)
        load_scale_rows(nc.sync, tab_scale_rows, tab_scales, True)
        picked_scale_rows = staged([P, S], U8, "picked_scale_rows", "room_f")
        nc.vector.tensor_copy(picked_scale_rows[:], tab_scale_rows[:].indirect(idx[:]))
        for a in range(2):
            nc.scalar.dma_start(
                out=v_scales[a][0:100, :].bitcast(I32), in_=picked_scale_rows[24 + 4 * a : 124 + 4 * a, :].bitcast(I32)
            )
        tab = [staged([P, T], U16, f"tab{a}", ("room_a", "room_b")[a]) for a in range(2)]
        for a in range(2):
            nc.sync.dma_start(out=tab[a][:].bitcast(I32), in_=tab_words[a].bitcast(I32))

        def load_w2(b, room):
            raw = staged([P, 2, PASS], I32, f"w2_raw{b}", room)
            nc.sync.dma_start(
                out=raw[:],
                in_=w2_words[:, :, PASS * b : PASS * (b + 1), :].rearrange("a p c i -> p a (c i)").bitcast(I32),
            )
            return raw

        w1_raw = {(0, 0): load_weight(w1, 0, 0, PASS, "room_d")}
        load_scale_rows(nc.sync, w2_scale_rows, w2_scales, False)
        w2_raw = [load_w2(0, "room_e")]
        w1_last = [load_weight(w1, 1, 256 * u, 256 * (u + 1), f"w1_last{u}") for u in range(2)]
        p2 = lists.tile([P, M // 16], U16, name="p2")
        nc.sync.dma_start(p2[:], pos2)
        p1 = lists.tile([P, M // 16], U16, name="p1")
        nc.sync.dma_start(p1[:], pos1)

        warm = held([P, 2], F32, "warm")
        nc.vector.memset(warm[:, 0:1], 0.0)
        nc.scalar.activation(out=warm[:, 1:2], in_=warm[:, 0:1], func=ACT.Tanh)

        v_words = [held([P, S], U16, f"v_words{a}") for a in range(2)]
        for a in range(2):
            nc.vector.tensor_copy(v_words[a][:], tab[a][:].indirect(idx[:]))
        w1_raw[0, 1] = load_weight(w1, 0, PASS, 2 * PASS, "room_a")
        w1_raw[1, 1] = load_weight(w1, 1, PASS, 2 * PASS, "room_b")
        w2_raw.append(load_w2(1, "room_c"))
        gains = staged([P, 2, PACK], F32, "gains", "room_f")
        nc.sync.dma_start(out=gains[:], in_=gain.rearrange("(b p t) -> p b t", b=2, t=PACK))

        w1_grouped = {(a, 0): staged([P, PASS * PACK], BF16, "grouped", f"grouped{a}") for a in range(2)}
        w1_q = {}
        w2_q = {}

        def deal_w2(b):
            words = staged([P, 2, PASS], I32, f"w2_dealt{b}", ("w2_dealt", "grouped0")[b])
            nc.vector.tensor_copy(
                out=words[:].rearrange("p a (t g i) -> p a g t i", t=PACK, i=4),
                in_=w2_raw[b][:].rearrange("p a (g i t) -> p a g t i", t=PACK, i=4),
            )
            scales = held([P, 2, PASS], U8, f"w2_dealt_scales{b}")
            nc.vector.tensor_copy(
                out=scales[:].rearrange("p a (t q) -> p a t q", t=PACK),
                in_=w2_scale_rows[:, :, PASS * b : PASS * (b + 1)].rearrange("p a (q t) -> p a t q", t=PACK),
            )
            for a in range(2):
                w2_q[a, b] = (words[:, a, :], scales[:, a, :])

        deal_w2(0)
        round_weight(nc.scalar.copy, w1_raw[0, 0], w1_grouped[0, 0][:], 0, P)
        round_weight(nc.scalar.copy, w1_last[0], w1_grouped[1, 0][:], 0, P // 2)
        round_weight(nc.vector.tensor_copy, w1_last[1], w1_grouped[1, 0][:], P // 2, P, P // 2)
        for a in range(2):
            w1_q[a, 0] = operand_tiles(f"w1_{a}0")
        for c0 in (0, PASS // 2):
            for a in range(2):
                quantize_part(w1_q[a, 0], w1_grouped[a, 0][:], c0, c0 + PASS // 2)

        w3_raw = [load_weight(w3, 0, 0, N, "room_d")]
        w4_raw = staged([P, 2, 2 * N], U8, "w4_raw", "room_e")
        nc.sync.dma_start(out=w4_raw[:].bitcast(I32), in_=w4_words.rearrange("a p c -> p a c").bitcast(I32))
        w4_scale_rows = staged([P, 2, N], U8, "w4_scale_rows", "w1_last0")
        nc.gpsimd.memset(w4_scale_rows[:].bitcast(I32), 0)
        load_scale_rows(nc.sync, w4_scale_rows, w4_scales, False)
        biases = staged([P, PACK], F32, "biases", "w1_last1")
        nc.sync.dma_start(out=biases[:], in_=b3.rearrange("(p t) -> p t", t=PACK))
        depths = staged([P, PACK], F32, "depths", "grouped1")
        nc.sync.dma_start(out=depths[:], in_=depth.rearrange("(p t) -> p t", t=PACK))
        w3_q = {}
        w4_q = {}

        def deal_w4():
            words = staged([P, 2, 2 * N], U8, "w4_dealt", "right41")
            nc.vector.tensor_copy(
                out=words[:].bitcast(U16).rearrange("p a (t q) -> p a t q", t=PACK),
                in_=w4_raw[:].bitcast(U16).rearrange("p a (q t) -> p a t q", t=PACK),
            )
            scales = staged([P, 2, N], U8, "w4_dealt_scales", "right1")
            nc.vector.tensor_copy(
                out=scales[:].rearrange("p a (t q) -> p a t q", t=PACK),
                in_=w4_scale_rows[:].rearrange("p a (q t) -> p a t q", t=PACK),
            )
            for b in range(2):
                w4_q[b] = (words[:, b, :], scales[:, b, :])

        stronger = [held([P, S], F32, f"stronger{i}") for i in range(8)]
        wear_rows = [held([P, PACK, M], BF16, f"wear_rows{b}") for b in range(2)]
        wear_grouped = [held([P, M * PACK], BF16, f"wear_grouped{b}") for b in range(2)]
        wear_codes = [held([P, M], U32, f"wear_codes{b}") for b in range(2)]
        wear_scales = [held([P, M], U8, f"wear_scales{b}") for b in range(2)]

        halves = [slice(0, BANK), slice(BANK, S)]
        right_copy = {}

        def product(i, weight, name):
            b, t = divmod(i, PACK)
            rows = slice(P * t, P * (t + 1))
            bank = [psum.tile([P, BANK], F32, name=name, tag=name) for cols in halves]
            for a in range(2):
                codes, scales = weight[a, b]
                for half, cols in enumerate(halves):
                    nc.tensor.matmul_mx(
                        out=bank[half][:], lhsT=codes[:, rows].bitcast(FP8X4), lhsT_scale=scales[:, rows],
                        rhs=v_words[a][:, cols].bitcast(FP4X4), rhs_scale=v_scales[a][:, cols],
                        start=(a == 0), stop=(a == 1),
                    )
            return bank

        def right_reading(i):
            if i == 4:
                parts = [staged([P, BANK], F32, "right_half", f"right4{half}") for half in range(2)]
                right_copy[i] = [part[:] for part in parts]
            else:
                whole = staged([P, S], F32, "right_copy", f"right{i}")
                right_copy[i] = [whole[:, cols] for cols in halves] + [whole[:]]
            for half, bank in enumerate(product(i, w2_q, "right")):
                nc.scalar.copy(out=right_copy[i][half], in_=bank[:])

        def left_reading(i):
            for half, bank in enumerate(product(i, w1_q, "left")):
                nc.vector.tensor_tensor(stronger[i][:, halves[half]], bank[:], right_copy[i][half], ALU.max)

        picked = {}

        def pick_catalogue(i, m0, m1, place):
            nc.vector.tensor_copy(place, stronger[i][:].indirect(p2[:, m0 // 16 : m1 // 16]))
            picked[i, m0] = place

        def pick_worn(i, m0, m1, place):
            b, t = divmod(i, PACK)
            nc.vector.tensor_tensor(place, stronger[i][:].indirect(p1[:, m0 // 16 : m1 // 16]), picked[i, m0], ALU.subtract)
            nc.scalar.activation(out=wear_rows[b][:, t, m0:m1], in_=place, func=ACT.Copy, scale=gains[:, b, t : t + 1])

        def group_wear(b, m0, m1):
            nc.scalar.copy(
                out=wear_grouped[b][:, PACK * m0 : PACK * m1].rearrange("p (g i t) -> p g t i", t=PACK, i=4),
                in_=wear_rows[b][:, :, m0:m1].rearrange("p t (g i) -> p g t i", i=4),
            )

        def quantize_wear(b, m0, m1):
            nc.vector.quantize_mx(
                out=wear_codes[b][:, m0:m1].bitcast(FP8X4), scales=wear_scales[b][:, m0:m1],
                in_=wear_grouped[b][:, PACK * m0 : PACK * m1],
            )

        def round_late(raw, i):
            grouped = right_copy[i][2].bitcast(BF16)
            for q0 in range(0, P, P // 4):
                round_weight(nc.scalar.copy, raw, grouped, q0, q0 + P // 4)
            return grouped

        right_reading(0)
        left_reading(0)
        right_reading(1)
        pick_catalogue(0, 0, M, held([P, M], F32, "catalogue0")[:])
        left_reading(1)
        right_reading(2)
        right_reading(3)
        deal_w2(1)
        grouped01 = round_late(w1_raw[0, 1], 0)
        w3_raw.append(load_weight(w3, 1, 0, N, "room_a"))
        left_reading(2)
        right_reading(4)
        pick_catalogue(1, 0, M, right_copy[2][0])
        pick_worn(0, 0, M, right_copy[2][1])
        grouped11 = round_late(w1_raw[1, 1], 1)
        w1_q[0, 1] = quantize(grouped01, "w1_01")
        left_reading(3)
        right_reading(5)
        pick_worn(1, 0, M, held([P, M], F32, "diff1")[:])
        w1_q[1, 1] = quantize(grouped11, "w1_11")
        left_reading(4)
        right_reading(6)
        pick_catalogue(2, 0, M, right_copy[4][0])
        w3_early = round_late(w3_raw[0], 3)
        left_reading(5)
        right_reading(7)
        pick_catalogue(3, 0, M, right_copy[5][0])
        pick_worn(2, 0, M, right_copy[5][1])
        deal_w4()
        w3_late = round_late(w3_raw[1], 0)
        left_reading(6)
        pick_worn(3, 0, M, right_copy[6][0])
        w3_q[0] = quantize(w3_early, "w3_0")
        group_wear(0, 0, M)
        left_reading(7)
        w3_q[1] = quantize(w3_late, "w3_1")
        quantize_wear(0, 0, M)

        chunks = [(0, 256), (256, 384), (384, 512)]
        banks = {}

        def second_stage(c, b):
            m0, m1 = chunks[c]
            width = m1 - m0
            per_bank = BANK // width
            for first in range(0, PACK, per_bank):
                if b == 0:
                    bounded = psum.tile([P, per_bank, width], F32, name="bounded", tag="right")
                    direct = psum.tile([P, per_bank, width], F32, name="direct", tag="left")
                    for u in range(per_bank):
                        banks[c, first + u] = (bounded[:, u, :], direct[:, u, :])
                for t in range(first, first + per_bank):
                    rows = slice(P * t, P * (t + 1))
                    codes, scales = w3_q[b]
                    nc.tensor.matmul_mx(
                        out=banks[c, t][0], lhsT=codes[:, rows].bitcast(FP8X4), lhsT_scale=scales[:, rows],
                        rhs=wear_codes[b][:, m0:m1].bitcast(FP8X4), rhs_scale=wear_scales[b][:, m0:m1],
                        start=(b == 0 and t == first), stop=(b == 1 and t == first + per_bank - 1),
                    )
                for t in range(first, first + per_bank):
                    rows = slice(P * t, P * (t + 1))
                    words, scales = w4_q[b]
                    for s in range(0, width, P):
                        cols = slice(m0 + s, m0 + s + P)
                        nc.tensor.matmul_mx(
                            out=banks[c, t][1][:, s : s + P],
                            lhsT=words[:, 2 * P * t : 2 * P * (t + 1)].bitcast(FP4X4), lhsT_scale=scales[:, rows],
                            rhs=wear_codes[b][:, cols].bitcast(FP8X4), rhs_scale=wear_scales[b][:, cols],
                            start=(b == 0 and t == first and s == 0),
                            stop=(b == 1 and t == first + per_bank - 1 and s == width - P),
                        )

        y_codes = held([P, M], U32, "y_codes")
        y_scales = held([P, M], U8, "y_scales")
        y_rows = out_0.rearrange("(p t) m -> p t m", t=PACK)
        y = [held([P, PACK, m1 - m0], F32, f"y{m0}") for m0, m1 in chunks]
        y_grouped = [held([P, (m1 - m0) * PACK], BF16, f"y_grouped{m0}") for m0, m1 in chunks]

        def finish(c, copy):
            m0, m1 = chunks[c]
            for t in range(PACK):
                bounded, direct = banks[c, t]
                squashed = ring.tile([P, m1 - m0], F32, name="squashed")
                nc.scalar.activation(out=squashed[:], in_=bounded, func=ACT.Tanh, bias=biases[:, t : t + 1])
                nc.vector.scalar_tensor_tensor(y[c][:, t, :], squashed[:], depths[:, t : t + 1], direct, ALU.mult, ALU.add)
            nc.sync.dma_start(out=y_rows[:, :, m0:m1], in_=y[c][:])
            copy(
                out=y_grouped[c][:].rearrange("p (g i t) -> p g t i", t=PACK, i=4),
                in_=y[c][:].rearrange("p t (g i) -> p g t i", i=4),
            )

        def planes(c):
            m0, m1 = chunks[c]
            nc.vector.quantize_mx(out=y_codes[:, m0:m1].bitcast(FP8X4), scales=y_scales[:, m0:m1], in_=y_grouped[c][:])
            nc.sync.dma_start(
                out=out_1[0].rearrange("p m t -> p (m t)")[:, PACK * m0 : PACK * m1].bitcast(I32),
                in_=y_codes[:, m0:m1].bitcast(I32),
            )

        def pick_chunk(c, room):
            m0, m1 = chunks[c]
            width = m1 - m0
            for t in range(PACK + 1):
                if t < PACK:
                    pick_catalogue(PACK + t, m0, m1, room(t))
                if t > 0:
                    diff = ring.tile([P, width], F32, name="diff")
                    pick_worn(PACK + t - 1, m0, m1, diff[:])
            group_wear(1, m0, m1)

        for c in range(3):
            second_stage(c, 0)
        pick_chunk(0, lambda t: right_copy[7][2][:, 256 * t : 256 * (t + 1)])
        pick_chunk(1, lambda t: right_copy[7][2][:, 256 * t : 256 * t + P])
        quantize_wear(1, *chunks[0])
        second_stage(0, 1)
        freed = wear_grouped[1][:, 0 : PACK * 256].bitcast(F32)
        pick_chunk(2, lambda t: freed[:, P * t : P * (t + 1)])
        quantize_wear(1, *chunks[1])
        second_stage(1, 1)
        finish(0, nc.vector.tensor_copy)
        quantize_wear(1, *chunks[2])
        second_stage(2, 1)
        finish(1, nc.vector.tensor_copy)
        planes(0)
        finish(2, nc.vector.tensor_copy)
        planes(1)
        planes(2)
        for quad in range(4):
            queue = nc.sync if quad % 2 == 0 else nc.scalar
            queue.dma_start(
                out=out_2[0, 4 * quad : 4 * quad + 4, :].bitcast(I32),
                in_=y_scales[32 * quad : 32 * quad + 4, :].bitcast(I32),
            )
